import numpy as np
import ml_dtypes

BF16 = ml_dtypes.bfloat16


def bf(x):
    return np.asarray(x, np.float32).astype(BF16)


def f32(x):
    return np.asarray(x, np.float32)


def f64(x):
    return np.asarray(x).astype(np.float64)


def striped(idx):
    return np.tile(idx.reshape(-1, 16).T, (8, 1))


S, K, M, N = 512, 128, 256, 64


def setup_inputs():
    return {"base": bf(np.random.standard_normal((M, S))), "x": bf(np.random.standard_normal((K, N))), "w": bf(np.random.standard_normal((K, M)) / np.sqrt(K)), "c": f32(0.2 + 0.8 * np.random.random_sample((1, S))), "offs": striped(np.random.permutation(S)[:N])}


def reference(base, x, w, c, offs):
    idx = offs[:16].T.reshape(-1)
    z = f64(base).copy()
    z[:, idx] = f64(w).T @ f64(x)
    return z * f64(c)

@@ -1,0 +1,56 @@
+import concourse.mybir as mybir
+from concourse.masks import make_identity
+
+BF16, F32, U16 = mybir.dt.bfloat16, mybir.dt.float32, mybir.dt.uint16
+
+P = 128
+S = 512
+N = 64
+M = 256
+BLOCKS = M // P
+
+FLOPS = 2 * P * M * N
+
+
+def tile_scatter_matmul_kernel(tc, base, x, w, c, offs, out):
+    nc = tc.nc
+    with (
+        tc.tile_pool(name="held", bufs=1) as held,
+        tc.psum_pool(name="banks", bufs=1) as banks,
+    ):
+        offsets = held.tile([P, N // 16], U16, name="offsets")
+        nc.sync.dma_start(offsets[:], offs)
+
+        base_rows = [held.tile([P, S], BF16, name="base_rows%d" % b) for b in range(BLOCKS)]
+        nc.sync.dma_start(base_rows[0][:], base[0:P, :])
+        nc.scalar.dma_start(base_rows[1][:], base[P : 2 * P, :])
+
+        weights = held.tile([P, M], BF16, name="weights")
+        nc.scalar.dma_start(weights[:], w)
+        moving = held.tile([P, N], BF16, name="moving")
+        nc.sync.dma_start(moving[:], x)
+
+        factors = held.tile([P, S], F32, name="factors")
+        nc.sync.dma_start(factors[:], c.rearrange("o s -> (o s)").partition_broadcast(P))
+
+        ident = held.tile([P, P], BF16, name="ident")
+        make_identity(nc, ident[:])
+
+        windows = [banks.tile([P, S], F32, name="window%d" % b) for b in range(BLOCKS)]
+        for b in range(BLOCKS):
+            nc.tensor.matmul(windows[b][:], ident[:], base_rows[b][:], start=True, stop=True)
+
+        for b in range(BLOCKS):
+            nc.tensor.matmul(
+                windows[b][:].indirect(offsets[:]),
+                weights[:, b * P : (b + 1) * P],
+                moving[:],
+                start=True,
+                stop=True,
+            )
+
+        for b in range(BLOCKS):
+            scaled = held.tile([P, S], F32, name="scaled%d" % b)
+            nc.vector.tensor_tensor(scaled[:], windows[b][:], factors[:], mybir.AluOpType.mult)
+            store_queue = nc.sync if b % 2 == 0 else nc.scalar
+            store_queue.dma_start(out[b * P : (b + 1) * P, :], scaled[:])

@@ -9,6 +9,8 @@ N = 64
 M = 256
 BLOCKS = M // P
 
+HALF = S // 2
+
 FLOPS = 2 * P * M * N
 
 
@@ -18,12 +20,12 @@ def tile_scatter_matmul_kernel(tc, base, x, w, c, offs, out):
         tc.tile_pool(name="held", bufs=1) as held,
         tc.psum_pool(name="banks", bufs=1) as banks,
     ):
-        offsets = held.tile([P, N // 16], U16, name="offsets")
-        nc.sync.dma_start(offsets[:], offs)
-
         base_rows = [held.tile([P, S], BF16, name="base_rows%d" % b) for b in range(BLOCKS)]
         nc.sync.dma_start(base_rows[0][:], base[0:P, :])
         nc.scalar.dma_start(base_rows[1][:], base[P : 2 * P, :])
+
+        offsets = held.tile([P, N // 16], U16, name="offsets")
+        nc.sync.dma_start(offsets[:], offs)
 
         weights = held.tile([P, M], BF16, name="weights")
         nc.scalar.dma_start(weights[:], w)
@@ -31,7 +33,7 @@ def tile_scatter_matmul_kernel(tc, base, x, w, c, offs, out):
         nc.sync.dma_start(moving[:], x)
 
         factors = held.tile([P, S], F32, name="factors")
-        nc.sync.dma_start(factors[:], c.rearrange("o s -> (o s)").partition_broadcast(P))
+        nc.scalar.dma_start(factors[:], c.rearrange("o s -> (o s)").partition_broadcast(P))
 
         ident = held.tile([P, P], BF16, name="ident")
         make_identity(nc, ident[:])
@@ -51,6 +53,8 @@ def tile_scatter_matmul_kernel(tc, base, x, w, c, offs, out):
 
         for b in range(BLOCKS):
             scaled = held.tile([P, S], F32, name="scaled%d" % b)
-            nc.vector.tensor_tensor(scaled[:], windows[b][:], factors[:], mybir.AluOpType.mult)
-            store_queue = nc.sync if b % 2 == 0 else nc.scalar
-            store_queue.dma_start(out[b * P : (b + 1) * P, :], scaled[:])
+            for h in range(2):
+                cols = slice(h * HALF, (h + 1) * HALF)
+                nc.vector.tensor_tensor(scaled[:, cols], windows[b][:, cols], factors[:, cols], mybir.AluOpType.mult)
+                store_queue = nc.sync if h == 0 else nc.scalar
+                store_queue.dma_start(out[b * P : (b + 1) * P, cols], scaled[:, cols])

@@ -20,12 +20,12 @@ def tile_scatter_matmul_kernel(tc, base, x, w, c, offs, out):
         tc.tile_pool(name="held", bufs=1) as held,
         tc.psum_pool(name="banks", bufs=1) as banks,
     ):
+        offsets = held.tile([P, N // 16], U16, name="offsets")
+        nc.sync.dma_start(offsets[:], offs)
+
         base_rows = [held.tile([P, S], BF16, name="base_rows%d" % b) for b in range(BLOCKS)]
         nc.sync.dma_start(base_rows[0][:], base[0:P, :])
         nc.scalar.dma_start(base_rows[1][:], base[P : 2 * P, :])
-
-        offsets = held.tile([P, N // 16], U16, name="offsets")
-        nc.sync.dma_start(offsets[:], offs)
 
         weights = held.tile([P, M], BF16, name="weights")
         nc.scalar.dma_start(weights[:], w)
@@ -33,7 +33,7 @@ def tile_scatter_matmul_kernel(tc, base, x, w, c, offs, out):
         nc.sync.dma_start(moving[:], x)
 
         factors = held.tile([P, S], F32, name="factors")
-        nc.scalar.dma_start(factors[:], c.rearrange("o s -> (o s)").partition_broadcast(P))
+        nc.sync.dma_start(factors[:], c.rearrange("o s -> (o s)").partition_broadcast(P))
 
         ident = held.tile([P, P], BF16, name="ident")
         make_identity(nc, ident[:])

@@ -9,8 +9,6 @@ N = 64
 M = 256
 BLOCKS = M // P
 
-HALF = S // 2
-
 FLOPS = 2 * P * M * N
 
 
@@ -24,13 +22,12 @@ def tile_scatter_matmul_kernel(tc, base, x, w, c, offs, out):
         nc.sync.dma_start(offsets[:], offs)
 
         base_rows = [held.tile([P, S], BF16, name="base_rows%d" % b) for b in range(BLOCKS)]
-        nc.sync.dma_start(base_rows[0][:], base[0:P, :])
-        nc.scalar.dma_start(base_rows[1][:], base[P : 2 * P, :])
-
-        weights = held.tile([P, M], BF16, name="weights")
-        nc.scalar.dma_start(weights[:], w)
+        for b in range(BLOCKS):
+            nc.sync.dma_start(base_rows[b][:], base[b * P : (b + 1) * P, :])
         moving = held.tile([P, N], BF16, name="moving")
         nc.sync.dma_start(moving[:], x)
+        weights = held.tile([P, M], BF16, name="weights")
+        nc.sync.dma_start(weights[:], w)
 
         factors = held.tile([P, S], F32, name="factors")
         nc.sync.dma_start(factors[:], c.rearrange("o s -> (o s)").partition_broadcast(P))
@@ -53,8 +50,5 @@ def tile_scatter_matmul_kernel(tc, base, x, w, c, offs, out):
 
         for b in range(BLOCKS):
             scaled = held.tile([P, S], F32, name="scaled%d" % b)
-            for h in range(2):
-                cols = slice(h * HALF, (h + 1) * HALF)
-                nc.vector.tensor_tensor(scaled[:, cols], windows[b][:, cols], factors[:, cols], mybir.AluOpType.mult)
-                store_queue = nc.sync if h == 0 else nc.scalar
-                store_queue.dma_start(out[b * P : (b + 1) * P, cols], scaled[:, cols])
+            nc.vector.tensor_tensor(scaled[:], windows[b][:], factors[:], mybir.AluOpType.mult)
+            nc.sync.dma_start(out[b * P : (b + 1) * P, :], scaled[:])

@@ -8,6 +8,7 @@ S = 512
 N = 64
 M = 256
 BLOCKS = M // P
+WARM_UPS = 4
 
 FLOPS = 2 * P * M * N
 
@@ -18,6 +19,12 @@ def tile_scatter_matmul_kernel(tc, base, x, w, c, offs, out):
         tc.tile_pool(name="held", bufs=1) as held,
         tc.psum_pool(name="banks", bufs=1) as banks,
     ):
+        zeros = held.tile([P, S], BF16, name="zeros")
+        nc.vector.memset(zeros[:], 0.0)
+        unread = banks.tile([P, S], F32, name="unread")
+        for repeat in range(WARM_UPS):
+            nc.tensor.matmul(unread[:], zeros[:, 0:P], zeros[:], start=True, stop=True)
+
         offsets = held.tile([P, N // 16], U16, name="offsets")
         nc.sync.dma_start(offsets[:], offs)
 

@@ -28,6 +28,9 @@ def tile_scatter_matmul_kernel(tc, base, x, w, c, offs, out):
         offsets = held.tile([P, N // 16], U16, name="offsets")
         nc.sync.dma_start(offsets[:], offs)
 
+        factor_row = held.tile([1, S], F32, name="factor_row")
+        nc.sync.dma_start(factor_row[:], c)
+
         base_rows = [held.tile([P, S], BF16, name="base_rows%d" % b) for b in range(BLOCKS)]
         for b in range(BLOCKS):
             nc.sync.dma_start(base_rows[b][:], base[b * P : (b + 1) * P, :])
@@ -36,11 +39,15 @@ def tile_scatter_matmul_kernel(tc, base, x, w, c, offs, out):
         weights = held.tile([P, M], BF16, name="weights")
         nc.sync.dma_start(weights[:], w)
 
-        factors = held.tile([P, S], F32, name="factors")
-        nc.sync.dma_start(factors[:], c.rearrange("o s -> (o s)").partition_broadcast(P))
-
         ident = held.tile([P, P], BF16, name="ident")
         make_identity(nc, ident[:])
+
+        ones = held.tile([1, P], F32, name="ones")
+        nc.vector.memset(ones[:], 1.0)
+        spread = banks.tile([P, S], F32, name="spread")
+        nc.tensor.matmul(spread[:], ones[:], factor_row[:], start=True, stop=True)
+        factors = held.tile([P, S], F32, name="factors")
+        nc.vector.tensor_copy(factors[:], spread[:])
 
         windows = [banks.tile([P, S], F32, name="window%d" % b) for b in range(BLOCKS)]
         for b in range(BLOCKS):

@@ -8,7 +8,7 @@ S = 512
 N = 64
 M = 256
 BLOCKS = M // P
-WARM_UPS = 4
+WARM_UPS = 3
 
 FLOPS = 2 * P * M * N
 
@@ -19,11 +19,13 @@ def tile_scatter_matmul_kernel(tc, base, x, w, c, offs, out):
         tc.tile_pool(name="held", bufs=1) as held,
         tc.psum_pool(name="banks", bufs=1) as banks,
     ):
-        zeros = held.tile([P, S], BF16, name="zeros")
-        nc.vector.memset(zeros[:], 0.0)
-        unread = banks.tile([P, S], F32, name="unread")
+        zeros = held.tile([P, P], BF16, name="zeros")
+        nc.gpsimd.memset(zeros[:], 0.0)
+        unread = banks.tile([P, S // P, P], F32, name="unread")
         for repeat in range(WARM_UPS):
-            nc.tensor.matmul(unread[:], zeros[:, 0:P], zeros[:], start=True, stop=True)
+            nc.tensor.matmul(
+                unread[:], zeros[:], zeros[:].unsqueeze(1).to_broadcast([P, S // P, P]), start=True, stop=True
+            )
 
         offsets = held.tile([P, N // 16], U16, name="offsets")
         nc.sync.dma_start(offsets[:], offs)

@@ -8,7 +8,7 @@ S = 512
 N = 64
 M = 256
 BLOCKS = M // P
-WARM_UPS = 3
+WARM_UPS = 2
 
 FLOPS = 2 * P * M * N
 
@@ -30,8 +30,8 @@ def tile_scatter_matmul_kernel(tc, base, x, w, c, offs, out):
         offsets = held.tile([P, N // 16], U16, name="offsets")
         nc.sync.dma_start(offsets[:], offs)
 
-        factor_row = held.tile([1, S], F32, name="factor_row")
-        nc.sync.dma_start(factor_row[:], c)
+        factor_columns = held.tile([P, S // P], F32, name="factor_columns")
+        nc.sync.dma_start(factor_columns[:], c.rearrange("o (p a) -> p (o a)", a=S // P))
 
         base_rows = [held.tile([P, S], BF16, name="base_rows%d" % b) for b in range(BLOCKS)]
         for b in range(BLOCKS):
@@ -41,15 +41,18 @@ def tile_scatter_matmul_kernel(tc, base, x, w, c, offs, out):
         weights = held.tile([P, M], BF16, name="weights")
         nc.sync.dma_start(weights[:], w)
 
+        ident32 = held.tile([P, P], F32, name="ident32")
+        make_identity(nc, ident32[:])
+        spread = banks.tile([P, S // P, P], F32, name="spread")
+        for a in range(S // P):
+            nc.tensor.transpose(spread[:, a, :], factor_columns[:, a : a + 1].to_broadcast([P, P]), ident32[:])
+        factors = held.tile([P, S], F32, name="factors")
+        nc.vector.tensor_copy(
+            factors[:].rearrange("m (p a) -> m p a", a=S // P), spread[:].rearrange("m a p -> m p a")
+        )
+
         ident = held.tile([P, P], BF16, name="ident")
         make_identity(nc, ident[:])
-
-        ones = held.tile([1, P], F32, name="ones")
-        nc.vector.memset(ones[:], 1.0)
-        spread = banks.tile([P, S], F32, name="spread")
-        nc.tensor.matmul(spread[:], ones[:], factor_row[:], start=True, stop=True)
-        factors = held.tile([P, S], F32, name="factors")
-        nc.vector.tensor_copy(factors[:], spread[:])
 
         windows = [banks.tile([P, S], F32, name="window%d" % b) for b in range(BLOCKS)]
         for b in range(BLOCKS):

@@ -27,9 +27,6 @@ def tile_scatter_matmul_kernel(tc, base, x, w, c, offs, out):
                 unread[:], zeros[:], zeros[:].unsqueeze(1).to_broadcast([P, S // P, P]), start=True, stop=True
             )
 
-        offsets = held.tile([P, N // 16], U16, name="offsets")
-        nc.sync.dma_start(offsets[:], offs)
-
         factor_columns = held.tile([P, S // P], F32, name="factor_columns")
         nc.sync.dma_start(factor_columns[:], c.rearrange("o (p a) -> p (o a)", a=S // P))
 
@@ -41,8 +38,13 @@ def tile_scatter_matmul_kernel(tc, base, x, w, c, offs, out):
         weights = held.tile([P, M], BF16, name="weights")
         nc.sync.dma_start(weights[:], w)
 
+        offsets = held.tile([P, N // 16], U16, name="offsets")
+        nc.sync.dma_start(offsets[:], offs)
+
         ident32 = held.tile([P, P], F32, name="ident32")
         make_identity(nc, ident32[:])
+        ident = held.tile([P, P], BF16, name="ident")
+        nc.vector.tensor_copy(ident[:], ident32[:])
         spread = banks.tile([P, S // P, P], F32, name="spread")
         for a in range(S // P):
             nc.tensor.transpose(spread[:, a, :], factor_columns[:, a : a + 1].to_broadcast([P, P]), ident32[:])
@@ -50,9 +52,6 @@ def tile_scatter_matmul_kernel(tc, base, x, w, c, offs, out):
         nc.vector.tensor_copy(
             factors[:].rearrange("m (p a) -> m p a", a=S // P), spread[:].rearrange("m a p -> m p a")
         )
-
-        ident = held.tile([P, P], BF16, name="ident")
-        make_identity(nc, ident[:])
 
         windows = [banks.tile([P, S], F32, name="window%d" % b) for b in range(BLOCKS)]
         for b in range(BLOCKS):

@@ -20,7 +20,7 @@ def tile_scatter_matmul_kernel(tc, base, x, w, c, offs, out):
         tc.psum_pool(name="banks", bufs=1) as banks,
     ):
         zeros = held.tile([P, P], BF16, name="zeros")
-        nc.gpsimd.memset(zeros[:], 0.0)
+        nc.vector.memset(zeros[:], 0.0)
         unread = banks.tile([P, S // P, P], F32, name="unread")
         for repeat in range(WARM_UPS):
             nc.tensor.matmul(
@@ -42,7 +42,8 @@ def tile_scatter_matmul_kernel(tc, base, x, w, c, offs, out):
         nc.sync.dma_start(offsets[:], offs)
 
         ident32 = held.tile([P, P], F32, name="ident32")
-        make_identity(nc, ident32[:])
+        nc.vector.memset(ident32[:], 0.0)
+        make_identity(nc, ident32[:], nomemset=True)
         ident = held.tile([P, P], BF16, name="ident")
         nc.vector.tensor_copy(ident[:], ident32[:])
         spread = banks.tile([P, S // P, P], F32, name="spread")

@@ -33,13 +33,12 @@ def tile_scatter_matmul_kernel(tc, base, x, w, c, offs, out):
         base_rows = [held.tile([P, S], BF16, name="base_rows%d" % b) for b in range(BLOCKS)]
         for b in range(BLOCKS):
             nc.sync.dma_start(base_rows[b][:], base[b * P : (b + 1) * P, :])
-        moving = held.tile([P, N], BF16, name="moving")
-        nc.sync.dma_start(moving[:], x)
-        weights = held.tile([P, M], BF16, name="weights")
-        nc.sync.dma_start(weights[:], w)
-
         offsets = held.tile([P, N // 16], U16, name="offsets")
         nc.sync.dma_start(offsets[:], offs)
+        weights = held.tile([P, M], BF16, name="weights")
+        nc.sync.dma_start(weights[:], w)
+        moving = held.tile([P, N], BF16, name="moving")
+        nc.sync.dma_start(moving[:], x)
 
         ident32 = held.tile([P, P], F32, name="ident32")
         nc.vector.memset(ident32[:], 0.0)

@@ -8,7 +8,7 @@ S = 512
 N = 64
 M = 256
 BLOCKS = M // P
-WARM_UPS = 2
+WARM_UPS = 3
 
 FLOPS = 2 * P * M * N
 

@@ -45,13 +45,13 @@ def tile_scatter_matmul_kernel(tc, base, x, w, c, offs, out):
         make_identity(nc, ident32[:], nomemset=True)
         ident = held.tile([P, P], BF16, name="ident")
         nc.vector.tensor_copy(ident[:], ident32[:])
-        spread = banks.tile([P, S // P, P], F32, name="spread")
-        for a in range(S // P):
-            nc.tensor.transpose(spread[:, a, :], factor_columns[:, a : a + 1].to_broadcast([P, P]), ident32[:])
-        factors = held.tile([P, S], F32, name="factors")
-        nc.vector.tensor_copy(
-            factors[:].rearrange("m (p a) -> m p a", a=S // P), spread[:].rearrange("m a p -> m p a")
-        )
+        spread = [banks.tile([P, 2, P], F32, name="spread%d" % g) for g in range(2)]
+        factors = held.tile([P, 2, P, 2], F32, name="factors")
+        for g in range(2):
+            for e in range(2):
+                a = 2 * g + e
+                nc.tensor.transpose(spread[g][:, e, :], factor_columns[:, a : a + 1].to_broadcast([P, P]), ident32[:])
+            nc.vector.tensor_copy(factors[:, g, :, :], spread[g][:].rearrange("m e p -> m p e"))
 
         windows = [banks.tile([P, S], F32, name="window%d" % b) for b in range(BLOCKS)]
         for b in range(BLOCKS):
@@ -68,5 +68,10 @@ def tile_scatter_matmul_kernel(tc, base, x, w, c, offs, out):
 
         for b in range(BLOCKS):
             scaled = held.tile([P, S], F32, name="scaled%d" % b)
-            nc.vector.tensor_tensor(scaled[:], windows[b][:], factors[:], mybir.AluOpType.mult)
+            nc.vector.tensor_tensor(
+                scaled[:].rearrange("m (p g e) -> m p g e", g=2, e=2),
+                windows[b][:].rearrange("m (p g e) -> m p g e", g=2, e=2),
+                factors[:].rearrange("m g p e -> m p g e"),
+                mybir.AluOpType.mult,
+            )
             nc.sync.dma_start(out[b * P : (b + 1) * P, :], scaled[:])

@@ -19,12 +19,16 @@ def tile_scatter_matmul_kernel(tc, base, x, w, c, offs, out):
         tc.tile_pool(name="held", bufs=1) as held,
         tc.psum_pool(name="banks", bufs=1) as banks,
     ):
-        zeros = held.tile([P, P], BF16, name="zeros")
+        zeros = held.tile([P, 2], BF16, name="zeros")
         nc.vector.memset(zeros[:], 0.0)
-        unread = banks.tile([P, S // P, P], F32, name="unread")
+        unread = banks.tile([P, S], F32, name="unread")
         for repeat in range(WARM_UPS):
             nc.tensor.matmul(
-                unread[:], zeros[:], zeros[:].unsqueeze(1).to_broadcast([P, S // P, P]), start=True, stop=True
+                unread[:],
+                zeros[:, 0:1].to_broadcast([P, P]),
+                zeros[:, 0:1].to_broadcast([P, S]),
+                start=True,
+                stop=True,
             )
 
         factor_columns = held.tile([P, S // P], F32, name="factor_columns")

import concourse.mybir as mybir
from concourse.masks import make_identity

BF16, F32, U16 = mybir.dt.bfloat16, mybir.dt.float32, mybir.dt.uint16

P = 128
S = 512
N = 64
M = 256
BLOCKS = M // P
WARM_UPS = 3

FLOPS = 2 * P * M * N


def tile_scatter_matmul_kernel(tc, base, x, w, c, offs, out):
    nc = tc.nc
    with (
        tc.tile_pool(name="held", bufs=1) as held,
        tc.psum_pool(name="banks", bufs=1) as banks,
    ):
        zeros = held.tile([P, 2], BF16, name="zeros")
        nc.vector.memset(zeros[:], 0.0)
        unread = banks.tile([P, S], F32, name="unread")
        for repeat in range(WARM_UPS):
            nc.tensor.matmul(
                unread[:],
                zeros[:, 0:1].to_broadcast([P, P]),
                zeros[:, 0:1].to_broadcast([P, S]),
                start=True,
                stop=True,
            )

        factor_columns = held.tile([P, S // P], F32, name="factor_columns")
        nc.sync.dma_start(factor_columns[:], c.rearrange("o (p a) -> p (o a)", a=S // P))

        base_rows = [held.tile([P, S], BF16, name="base_rows%d" % b) for b in range(BLOCKS)]
        for b in range(BLOCKS):
            nc.sync.dma_start(base_rows[b][:], base[b * P : (b + 1) * P, :])
        offsets = held.tile([P, N // 16], U16, name="offsets")
        nc.sync.dma_start(offsets[:], offs)
        weights = held.tile([P, M], BF16, name="weights")
        nc.sync.dma_start(weights[:], w)
        moving = held.tile([P, N], BF16, name="moving")
        nc.sync.dma_start(moving[:], x)

        ident32 = held.tile([P, P], F32, name="ident32")
        nc.vector.memset(ident32[:], 0.0)
        make_identity(nc, ident32[:], nomemset=True)
        ident = held.tile([P, P], BF16, name="ident")
        nc.vector.tensor_copy(ident[:], ident32[:])
        spread = [banks.tile([P, 2, P], F32, name="spread%d" % g) for g in range(2)]
        factors = held.tile([P, 2, P, 2], F32, name="factors")
        for g in range(2):
            for e in range(2):
                a = 2 * g + e
                nc.tensor.transpose(spread[g][:, e, :], factor_columns[:, a : a + 1].to_broadcast([P, P]), ident32[:])
            nc.vector.tensor_copy(factors[:, g, :, :], spread[g][:].rearrange("m e p -> m p e"))

        windows = [banks.tile([P, S], F32, name="window%d" % b) for b in range(BLOCKS)]
        for b in range(BLOCKS):
            nc.tensor.matmul(windows[b][:], ident[:], base_rows[b][:], start=True, stop=True)

        for b in range(BLOCKS):
            nc.tensor.matmul(
                windows[b][:].indirect(offsets[:]),
                weights[:, b * P : (b + 1) * P],
                moving[:],
                start=True,
                stop=True,
            )

        for b in range(BLOCKS):
            scaled = held.tile([P, S], F32, name="scaled%d" % b)
            nc.vector.tensor_tensor(
                scaled[:].rearrange("m (p g e) -> m p g e", g=2, e=2),
                windows[b][:].rearrange("m (p g e) -> m p g e", g=2, e=2),
                factors[:].rearrange("m g p e -> m p g e"),
                mybir.AluOpType.mult,
            )
            nc.sync.dma_start(out[b * P : (b + 1) * P, :], scaled[:])
